import numpy as np, ml_dtypes
CORES = [23,119,17,113]
N = 4
BF = ml_dtypes.bfloat16
P, TW, M, RO = 4096, 4096, 3, 4
def parts(rng):
    v = rng.integers(0, 128, (N, 8, 16, P)); v[:, :, 15] = rng.integers(0, 2, (N, 8, P))
    t = rng.integers(0, 128, (N, 8, 16, TW)); t[:, :, 15] = rng.integers(0, 2, (N, 8, TW))
    return v, t, rng.integers(1, 256, (N, 8, 16)), rng.integers(0, 2048, (N, 8, RO, M))
def pack(v, t, w, k):
    return {"x": v.reshape(N, 128, P).astype(np.float32).astype(BF), "tm": t.reshape(N, 128, TW).astype(np.float32).astype(BF),
            "wt": np.ascontiguousarray(w.reshape(N, 128, 1)).astype(np.int32),
            "km": np.repeat(k.reshape(N, 8, 1, RO * M), 16, axis=2).reshape(N, 128, RO * M).astype(np.int32)}
def aim(rng, q, noth):
    u = np.arange(1, 4096, 2); i = u.copy()
    for _ in range(4): i = (i * (2 - u * i)) & 4095
    kk = ((q - (u * u >> 5)) * i) & (P - 1)
    ok = np.flatnonzero((kk < 2048) & (((u * u >> 4) & (TW - 1)) != noth))
    s = int(rng.choice(ok)); return int(u[s]), int(kk[s])
def column(rng, w, u, s):
    c = rng.integers(0, 128, 16); c[15] = s; c[:2] = 0
    z = (u - int(np.sum(w * c))) & 4095; c[0] = z & 63; c[1] = z >> 6
    return c
def setup_inputs(rng):
    return pack(*parts(rng))
def setup_inputs_ends(rng):
    v, t, w, k = parts(rng); w[:, :, 0] = 1; w[:, :, 1] = 64; w[:, :, 15] = 0
    for r in range(N):
        o = (r + 1) % N
        for g in range(8):
            case = (g - r) % 9
            a = int(rng.integers(1, P // 4)); b = int(rng.integers(P // 2, 3 * P // 4))
            if case < 2: a, b = 0, P - 1
            if case in (2, 3): b = a + 1
            if case == 8: a, b = int(rng.integers(1, P // 8)), int(rng.integers(7 * P // 8, P - 8))
            p, q = a, b
            if case == 7 or (case < 6 and rng.random() < 0.5): p, q = b, a
            s = int(rng.integers(0, 2)); u, k[r, g, 0, 0] = aim(rng, q, -1); c = column(rng, w[r, g], u, s); h = (u * u >> 4) & (TW - 1)
            if case == 4: v[r, g, 15] = s
            v[r, g, :, p] = c; v[r, g, :, q] = c
            if case in (0, 3): v[r, g, 15, q] = 1 - s
            t[o, g, :15, h] = c[:15]
            if case == 6: v[r, g, :, int(rng.integers(a + 1, b))] = c
            if case == 7: v[r, g, :, b + 3] = c
            if case in (1, 4, 5, 7, 8):
                p2, q2 = {1: (P // 3, P // 2), 4: (a + 1, P - 1), 5: (b - 1, b + 1), 7: (a + 2, b - 2), 8: (P // 2, P - 3)}[case]
                if (case == 4 and r % 2 == 0) or rng.random() < 0.5: p2, q2 = q2, p2
                u2, k[r, g, 0, 1] = aim(rng, q2, h); c2 = column(rng, w[r, g], u2, s if case == 4 else int(rng.integers(0, 2))); h2 = (u2 * u2 >> 4) & (TW - 1)
                v[r, g, :, p2] = c2; v[r, g, :, q2] = c2; t[o, g, :15, h2] = c2[:15]; t[o, g, 0, h2] = c2[0] ^ (2 if case == 8 else 1)
            if case == 8:
                ks = np.arange(2048); zs = ((u * u >> 5) + ks * u) & (P - 1)
                ks = ks[(zs > a) & (zs < b) & (zs != P // 2)]
                k[r, g, 0, 2] = int(rng.choice(ks)); z = ((u * u >> 5) + int(k[r, g, 0, 2]) * u) & (P - 1)
                cz = c.copy(); cz[0] = c[0] ^ 1; uz = (u + int(cz[0]) - int(c[0])) & 4095
                v[r, g, :, z] = cz; t[o, g, :15, (u * uz >> 4) & (TW - 1)] = c[:15]
    return pack(v, t, w, k)
def setup_inputs_kinds(rng):
    v, t, w, k = parts(rng); w[:] = w[:1].copy(); w[:, :, 15] = 0
    for g in (0, 2, 4):
        w[:, g, 0] = 1; w[:, g, 1] = 64; w[:, g, (2 if g == 2 else 8):] = 0
        u = 3 if g == 4 else 2 * int(rng.integers(0, 2048)) + 1; c = column(rng, w[0, g], u, 0)
        if g != 2: v[:, g, :8] = c[:8, None]
        else:
            v[:, g, :2] = c[:2, None]; v[:, g, 2:15] = rng.integers(0, 41, (N, 13, P)); k[:, g, 0] = k[:, g, 0, :1].copy()
            for r in range(N): v[r, g, 2:15, ((u * u >> 5) + int(k[r, g, 0, 0]) * u) & (P - 1)] = rng.integers(120, 128, 13)
    for g in (1, 3, 5, 6, 7):
        n = 5 if g % 2 else int(rng.integers(2, 6)); kd = rng.integers(0, 128, (16, n))
        if g % 2:
            kd[:, 4] = rng.integers(40, 88, 16)
            kd[:, :4] = kd[:, 4:] + rng.integers(8, 41, (16, 4)) * (2 * rng.integers(0, 2, (16, 4)) - 1)
        for r in range(N):
            kind = rng.integers(0, n, P)
            if g % 2:
                c = r % 4; uc, u4 = [int(np.sum(w[r, g] * kd[:, i])) & 4095 for i in (c, 4)]
                kind[((u4 * u4 >> 5) + k[r, g, 0] * u4) & (P - 1)] = c
                t[(r + 1) % N, g, :15, (uc * u4 >> 4) & (TW - 1)] = (kd[:15, c] + kd[:15, 4]) >> 1
            v[r, g] = kd[:, kind]
    v[:, :, 15] = rng.integers(0, 2, (N, 8, P))
    return pack(v, t, w, k)
def setup_inputs_void(rng):
    v, t, w, k = parts(rng); w[:, :, 0] = 1; w[:, :, 1] = 64; k[:, ::2] = k[:, ::2, :1, :1].copy()
    for g in (0, 6):
        v[:, g, 2:15] &= 3; t[:, g, :15] = 124 + (t[:, g, :15] & 3)
    us = np.arange(4096); j = np.arange(P)
    for r in range(N):
        for g in range(8):
            pre = np.full(P, -1); pre[((us * us >> 5) + int(k[r, g, 0, 0]) * us) & (P - 1)] = us
            z = (pre - np.sum(w[r, g, 2:, None] * v[r, g, 2:], axis=0)) & 4095
            v[r, g, 0] = np.where(pre >= 0, z & 63, v[r, g, 0]); v[r, g, 1] = np.where(pre >= 0, z >> 6, v[r, g, 1])
            if g in (0, 6):
                u = np.sum(w[r, g, :, None] * v[r, g], axis=0) & 4095; q = ((u * u >> 5) + int(k[r, g, 0, 0]) * u) & (P - 1)
                h = (u * u[q] >> 4) & (TW - 1); free = np.flatnonzero((q == j) & ~np.isin(h, h[q != j]))
                if len(free):
                    p = int(rng.choice(free)); t[(r + 1) % N, g, :15, int(h[p])] = v[r, g, :15, p]
    return pack(v, t, w, k)
def setup_inputs_small(rng):
    v, t, w, k = parts(rng)
    return pack(v & 1, t & 1, w, k)
def setup_inputs_spread(rng):
    v, t, w, k = parts(rng); both = []
    for a in (v, t):
        n = a.shape[-1]; b = np.minimum((np.exp2(8 * rng.random((N, 8, 1, n))) * rng.random(a.shape)).astype(np.int64), 127)
        z = rng.integers(0, 32, (N, 8, 1, n)); b = np.where(z == 0, 0, np.where(z == 1, 127, b)); b[:, :, 15] = a[:, :, 15]; both.append(b)
    w = np.minimum(np.exp2(8.1 * rng.random((N, 8, 16))).astype(np.int64), 255); w[:, :, 3] = 0; w[:, :, 4] = 255
    w[:, 5] = rng.integers(200, 256, (N, 16)); w[:, 6] = 255
    both[0][:, 5, :15] = rng.integers(100, 128, (N, 15, P)); both[0][:, 6, :15] = rng.integers(64, 128, (N, 15, P))
    both[0][:, 6, :15, P - 1] = 127; both[0][:, 6, 15, P - 1] = 1
    k = np.minimum(np.exp2(11.1 * rng.random((N, 8, RO, M))).astype(np.int64) - 1, 2047); k[:, 1, 0, 0] = 0; k[:, 2, 0, 1] = 2047
    return pack(both[0], both[1], w, k)
def check_inputs(d):
    bad = []
    for name in ("x", "tm"):
        a = np.asarray(d[name]).astype(np.float32)
        if not np.all((a >= 0) & (a <= 127) & (np.floor(a) == a)): bad.append("whole numbers of " + name)
        if not np.all(a[:, 15::16] <= 1): bad.append("signs of " + name)
    for name, hi in (("wt", 255), ("km", 2047)):
        if np.min(d[name]) < 0 or np.max(d[name]) > hi: bad.append("range of " + name)
    a = np.asarray(d["km"]); a = a.reshape(a.shape[0], 8, 16, -1)
    if not np.all(a == a[:, :, :1]): bad.append("rows of km alike")
    return bad
def reference(x, tm, wt, km):
    v = x.astype(np.float32).astype(np.int32).reshape(N, 8, 16, P); tp = tm.astype(np.float32).astype(np.int32).reshape(N, 8, 16, TW)
    w = wt.astype(np.int32).reshape(N, 8, 16, 1); k = km.astype(np.int32).reshape(N, 8, 16, RO, M)[:, :, 0]; j = np.arange(P)
    for t in range(RO):
        u = np.add.reduce(w * v, axis=2, dtype=np.int32) & 4095
        bq = bd = None
        for m in range(M):
            q = ((u * u >> 5) + k[:, :, t, m][:, :, None] * u) & (P - 1)
            xq = np.take_along_axis(v, q[:, :, None, :], 3)
            dm = np.where(q == j, 8192, np.add.reduce(np.abs(v - xq)[:, :, :15], axis=2))
            if m == 0: bq, bd = q, dm
            else: bq, bd = np.where(dm < bd, q, bq), np.minimum(bd, dm)
        xq = np.take_along_axis(v, bq[:, :, None, :], 3)
        h = (u * np.take_along_axis(u, bq, 2) >> 4) & (TW - 1)
        got = np.stack([np.take_along_axis(tp[(r + 1 + t % (N - 1)) % N], h[r][:, None, :], 2) for r in range(N)])
        e = bd + np.add.reduce(np.abs(v + xq - 2 * got)[:, :, :15], axis=2)
        alike = v[:, :, 15] == xq[:, :, 15]; lo = np.minimum(j, bq); hi = np.maximum(j, bq)
        nv = np.empty_like(v)
        for r in range(N):
            for g in range(8):
                p = int(np.argmin(e[r, g])); a, b = int(lo[r, g, p]), int(hi[r, g, p])
                z = v[r, g].copy(); z[:15, a] = (v[r, g, :15, a] + v[r, g, :15, b]) >> 1
                tp[r, g, :, int(h[r, g, p])] = z[:, a]
                if not alike[r, g, p]:
                    z[:, a + 1:b + 1] = z[:, a + 1:b + 1][:, ::-1].copy(); z[15, a + 1:b + 1] = 1 - z[15, a + 1:b + 1]
                else:
                    c, d = b, P - 1
                    inside = alike[r, g] & (lo[r, g] > a) & (lo[r, g] < b)
                    if np.any(inside):
                        p2 = int(np.argmin(np.where(inside, e[r, g], 2 ** 20)))
                        if hi[r, g, p2] > b: c, d = int(lo[r, g, p2]), int(hi[r, g, p2])
                    z = z[:, np.concatenate([j[:a + 1], j[b + 1:d + 1], j[c + 1:b + 1], j[a + 1:c + 1], j[d + 1:]])]
                nv[r, g] = z
        v = nv
    return {"y": v.reshape(N, 128, P).astype(np.float32).astype(BF)}

@@ -1,0 +1,625 @@
+from concourse.mybir import AluOpType, AxisListType, ActivationFunctionType
+
+P = 4096
+FO = P + 16
+XW = FO + P
+HALF = 2048
+HC = 128
+BANK = 512
+SDT = (1856, 672, 480, 384, 384, 512)
+SY = (576, 448)
+SET = (768, 448)
+YC = 1024
+CUT = (1024, 1472)
+RS = 2432
+VOID = 1920.0
+
+BF, F4, I4, U2 = "bfloat16", "float32", "int32", "uint16"
+SCRATCH = {"PS": ("psum", [128, 4096], F4)}
+for _names, _w, _d in ((("XB0", "XB1"), XW, BF), (("T1", "T2", "T3"), P + 16, BF), (("TMB", "YB", "ZB", "NX"), P, BF),
+                       (("AD0", "AD1", "AD2"), HALF, BF), (("XQ", "NA"), 1024, BF), (("SG1", "SG2", "VD"), 256, BF), (("EQ",), 768, BF),
+                       (("KM",), 12, I4), (("WT", "PIX", "II", "GI"), 1, I4), (("KMF",), 12, F4),
+                       (("WTF", "IF", "GF", "PF", "G15", "FM", "FM2", "SM", "I0", "PADC"), 1, F4),
+                       (("ROW", "Z0"), 144, F4), (("ROWI", "ROWG"), 128, I4), (("NB", "NF", "PN"), 256, F4),
+                       (("GM", "IDF", "I2K"), 128, F4), (("D16",), 16, F4), (("ZW", "ZD", "ZE", "ZS"), 144, BF),
+                       (("IB", "IN", "IEQ", "IVD"), 128, BF), (("UR", "U", "US", "V1", "KI", "IQ", "IH", "KD", "UQ", "UA", "UH"), 256, I4),
+                       (("QR", "QI"), 768, I4), (("QO",), 768, U2), (("QB",), 768, F4), (("QSO", "HO", "RO"), 256, U2),
+                       (("KA", "KB", "KF", "DIRT", "CC", "NN", "K2", "Y0", "Y1", "VA", "TA", "TB", "TC"), 256, F4),
+                       (("CF",), 64, F4), (("CI",), 16, I4), (("OFF",), 16, U2), (("R32",), 32, F4), (("GQ",), 64, F4),
+                       (("XA", "XC"), 16, F4), (("NI", "NJ"), 16, I4),
+                       (("UP0", "UP1", "UP2", "RU10", "RU11", "RU12", "RU20", "RU30", "RU31"), 32, F4)):
+    for _n in _names:
+        SCRATCH[_n] = ("sbuf", [128, _w], _d)
+UPD = [(1, 0), (2, 0), (3, 0), (1, 1), (3, 1), (1, 2)]
+SEMAPHORES = (["cv", "cs", "cp", "cg", "km", "wt", "xf", "sa", "sb", "ls"] + ["x%d" % i for i in range(4)] + ["tm%d" % i for i in range(2)]
+              + ["nx0", "nx1"] + ["y%d" % i for i in range(6)] + ["rt1", "rt2", "rt3"] + ["ru%d%d" % u for u in UPD])
+
+OP = AluOpType
+ACT = ActivationFunctionType
+COPY = ACT.Identity
+
+
+def r(name, c0, c1, step=1):
+    return ("r", name, c0, c1, step)
+
+
+def ind(win, off):
+    return ("i", win, off)
+
+
+def rank_program(g, core, T, topo):
+    rank = T.rank_of(core)
+    if rank is None:
+        return
+    N = len(T.cores)
+    queue = {"v": g.vector, "s": g.scalar, "p": g.tensor, "g": g, "y": g.sync}
+    own = {"v": "cv", "s": "cs", "p": "cp", "g": "cg"}
+    total = {}
+    clock = {q: {} for q in queue}
+    rec = {}
+    bank = {}
+    serial = [0]
+
+    def merge(a, b):
+        for k, v in b.items():
+            if a.get(k, 0) < v:
+                a[k] = v
+
+    def need(q, outs, ins):
+        deps = []
+        for (_, name, c0, c1, st) in ins:
+            for x in rec.get(name, []):
+                if x[2] and x[0] < c1 and c0 < x[1]:
+                    deps.append(x)
+        for (_, name, c0, c1, st) in outs:
+            for x in rec.get(name, []):
+                if x[0] < c1 and c0 < x[1] and not (x[3] == q and q == "p"):
+                    deps.append(x)
+        for (_, name, c0, c1, st) in list(outs) + list(ins):
+            if name == "PS":
+                for b in range(c0 // BANK, (c1 - 1) // BANK + 1):
+                    for q2, x in bank.get(b, {}).items():
+                        if q2 != q:
+                            deps.append(x)
+        ck = clock[q]
+        deps.sort(key=lambda x: -x[6])
+        todo = {}
+        for x in deps:
+            sem, val = x[4]
+            if ck.get(sem, 0) < val:
+                todo[sem] = max(todo.get(sem, 0), val)
+                merge(ck, x[5])
+        for sem, val in todo.items():
+            queue[q].wait_ge(T.sem[sem], val)
+
+    def note(q, ck, outs, ins, tok):
+        serial[0] += 1
+        snap = dict(ck)
+        merge(snap, {tok[0]: tok[1]})
+        for lst, w in ((ins, False), (outs, True)):
+            for (_, name, c0, c1, st) in lst:
+                new = (c0, c1, w, q, tok, snap, serial[0])
+                old = rec.get(name, [])
+                if w and st == 1:
+                    old = [x for x in old if not (c0 <= x[0] and x[1] <= c1)]
+                elif not w:
+                    old = [x for x in old if x[2] or x[3] != q or not (c0 <= x[0] and x[1] <= c1)]
+                old.append(new)
+                rec[name] = old
+                if name == "PS":
+                    for b in range(c0 // BANK, (c1 - 1) // BANK + 1):
+                        bank.setdefault(b, {})[q] = new
+
+    def ap(a):
+        if isinstance(a, tuple) and a and a[0] == "r":
+            return T[a[1]][:, a[2]:a[3]] if a[4] == 1 else T[a[1]][:, a[2]:a[3]:a[4]]
+        if isinstance(a, tuple) and a and a[0] == "i":
+            return ap(a[1]).indirect(ap(a[2]))
+        return a
+
+    def regs(a):
+        if isinstance(a, tuple) and a and a[0] == "r":
+            return [a]
+        if isinstance(a, tuple) and a and a[0] == "i":
+            return [a[1], a[2]]
+        return []
+
+    def bump(sem, n):
+        total[sem] = total.get(sem, 0) + n
+        return (sem, total[sem])
+
+    def E(q, call, out, *args, **kw):
+        outs = regs(out)
+        ins = outs[1:]
+        outs = outs[:1]
+        for a in list(args) + list(kw.values()):
+            ins = ins + regs(a)
+        need(q, outs, ins)
+        tok = bump(own[q], 1)
+        call(ap(out), *[ap(a) for a in args], **{k: ap(v) for k, v in kw.items()}).then_inc(T.sem[tok[0]], 1)
+        note(q, clock[q], outs, ins, tok)
+
+    def dma(q, sem, out_ap, in_ap, outs, ins):
+        need(q, outs, ins)
+        tok = bump(sem, 16)
+        queue[q].dma_start(out_ap, in_ap).then_inc(T.sem[sem], 16)
+        note(q + "dma", clock[q], outs, ins, tok)
+
+    def arrival(outs, tok):
+        note("remote", {}, outs, [], tok)
+
+    def ts(out, a, s1, s2, o0, o1=None):
+        if o1 is None:
+            E("v", g.vector.tensor_scalar, out, a, s1, None, o0)
+        else:
+            E("v", g.vector.tensor_scalar, out, a, s1, s2, o0, o1)
+
+    def tt(out, a, b, o):
+        E("v", g.vector.tensor_tensor, out, a, b, o)
+
+    def cp(out, a):
+        E("v", g.vector.tensor_copy, out, a)
+
+    def red(out, a):
+        E("v", g.vector.tensor_reduce, out, a, AxisListType.X, OP.min)
+
+    def act(out, a, f, **kw):
+        E("s", g.scalar.activation, out, a, f, **kw)
+
+    def mm(out, lhsT, rhs, start, stop):
+        E("p", g.tensor.matmul, out, lhsT, rhs, start, stop)
+
+    def ps(b, c0, c1):
+        return r("PS", b * BANK + c0, b * BANK + c1)
+
+    def cf(k):
+        return r("CF", k, k + 1)
+
+    def wsum(col, z, buf, c0, n, start, stop):
+        for i in range(16):
+            mm(r("PS", col, col + n // 16), r(z, 15 - i, 143 - i), r(buf, c0 + i, c0 + n, 16), start and i == 0, stop and i == 15)
+
+    U0, UQ0, SG0, PIX0 = (0, BANK + 128), (128, BANK + 256), 384, 2 * BANK + 384
+    K0 = (2 * BANK, 3 * BANK + 128)
+    KU0, KEY = 4 * BANK, 4 * BANK + 384
+    SMALL1, SMALL2 = 256, BANK + 384
+    CLAMP, YSUM = ps(7, 0, 256), ps(6, 256, 512)
+    PIXW = r("PS", PIX0, PIX0 + 256)
+
+    dma("s", "wt", T.WT[:], T.wt[:], [r("WT", 0, 1)], [])
+    dma("s", "km", T.KM[:], T.km[:], [r("KM", 0, 12)], [])
+    for i in range(4):
+        c = r("XB0", 1024 * i, 1024 * i + 1024)
+        dma("y", "x%d" % i, ap(c), T.x[:, 1024 * i:1024 * i + 1024], [c], [])
+    for i in range(2):
+        c = r("TMB", 2048 * i, 2048 * i + 2048)
+        dma("s", "tm%d" % i, ap(c), T.tm[:, 2048 * i:2048 * i + 2048], [c], [])
+    NXC = [HALF * h + min(SDT[3 * h:3 * h + 3] + SY[h:h + 1]) for h in (0, 1)]
+    for h in (0, 1):
+        c = r("NX", NXC[h], HALF * h + HALF)
+        dma("y", "nx%d" % h, ap(c), T.x[:, NXC[h]:HALF * h + HALF], [c], [])
+    E("g", g.iota, r("PIX", 0, 1), [[0, 1]], 0, 1)
+    E("g", g.iota, r("ROW", 0, 144), [[1, 144]], 0, 0, allow_small_or_imprecise_dtypes=True)
+    E("g", g.iota, r("NB", 0, 256), [[16, 256]], 0, 0, allow_small_or_imprecise_dtypes=True)
+    E("g", g.iota, r("ROWI", 0, 128), [[1, 128]], 0, 0)
+    for j in (1, 2, 3):
+        E("v", g.vector.memset, r("T%d" % j, P, P + 16), 0.0)
+    for j in (0, 1):
+        E("v", g.vector.memset, r("XB%d" % j, P, P + 16), 0.0)
+    for j in (0, 1, 2):
+        E("v", g.vector.memset, r("UP%d" % j, 0, 32), 0.0)
+    IF, PF, FM, INV15 = r("IF", 0, 1), r("PF", 0, 1), r("FM", 0, 1), r("SM", 0, 1)
+    Z0, ROWM = r("Z0", 0, 144), r("ROW", 0, 128)
+    ts(r("II", 0, 1), r("PIX", 0, 1), 15, None, OP.bitwise_and)
+    ts(r("GI", 0, 1), r("PIX", 0, 1), 4, None, OP.arith_shift_right)
+    cp(PF, r("PIX", 0, 1))
+    cp(IF, r("II", 0, 1))
+    cp(r("GF", 0, 1), r("GI", 0, 1))
+    cp(r("WTF", 0, 1), r("WT", 0, 1))
+    ts(r("G15", 0, 1), r("GF", 0, 1), 16.0, 15.0, OP.mult, OP.add)
+    ts(FM, IF, 14.5, None, OP.is_lt)
+    ts(INV15, IF, 14.5, None, OP.is_gt)
+    ts(Z0, r("ROW", 0, 144), r("G15", 0, 1), None, OP.is_equal)
+    ts(r("ZW", 0, 144), Z0, r("WTF", 0, 1), None, OP.mult)
+    cp(r("KMF", 0, 12), r("KM", 0, 12))
+    ts(r("NF", 0, 256), r("NB", 0, 256), IF, None, OP.add)
+    cp(PIXW, r("NF", 0, 256))
+    ts(r("IB", 0, 128), ROWM, PF, None, OP.is_equal)
+    ts(r("IN", 0, 128), ROWM, PF, -1.0, OP.is_equal, OP.mult)
+    ts(r("IEQ", 0, 128), ROWM, PF, VOID * 16384.0, OP.is_equal, OP.mult)
+    ts(r("IDF", 0, 128), ROWM, PF, None, OP.is_equal)
+    ts(r("ZD", 0, 144), Z0, FM, 16384.0, OP.mult, OP.mult)
+
+    sent = [0]
+
+    def send(dst, out_ap, in_reg, sem, use):
+        need("g", [], [in_reg])
+        rid, pid, _ = topo.addr(dst)
+        m = 0
+        for e in use:
+            m |= 1 << e
+        g.remote_dma(out_ap, ap(in_reg), T.sem[sem], T.sem["ls"], pid, rid, m)
+        sent[0] += len(use)
+
+    def lanes(src, dst):
+        e = topo.engines(src, dst)
+        if topo.chip(src) != topo.chip(dst):
+            return e
+        far = [topo.engines(src, c) for c in T.cores if topo.chip(c) != topo.chip(src)]
+        rest = [k for k in e if not any(k in f for f in far)]
+        return rest if rest else e
+
+    asker = {j: T.cores[(rank - j) % N] for j in (1, 2, 3)}
+    for j in (1, 2, 3):
+        n = len(lanes(T.cores[(rank + j) % N], core))
+        bump("rt%d" % j, n * (2 if j == 1 else 1))
+        arrival([r("T%d" % j, 0, P)], ("rt%d" % j, total["rt%d" % j]))
+        for (jj, t) in UPD:
+            if jj == j:
+                arrival([r("RU%d%d" % (j, t), 0, 32)], bump("ru%d%d" % (j, t), n))
+    for i in range(2):
+        c = r("TMB", 2048 * i, 2048 * i + 2048)
+        act(c, c, COPY, scale=2.0)
+        send(asker[1], T.T1[:, 2048 * i:2048 * i + 2048], c, "rt1", lanes(core, asker[1]))
+    send(asker[2], T.T2[:, 0:P], r("TMB", 0, P), "rt2", lanes(core, asker[2]))
+    send(asker[3], T.T3[:, 0:P], r("TMB", 0, P), "rt3", lanes(core, asker[3]))
+
+    def late_constants():
+        ts(r("D16", 0, 16), r("ROW", 0, 16), IF, None, OP.is_equal)
+        ts(r("ROWG", 0, 128), r("ROWI", 0, 128), 4, None, OP.arith_shift_right)
+        ts(r("ZE", 0, 144), Z0, FM, 2048.0, OP.mult, OP.mult)
+        ts(r("ZS", 0, 144), Z0, INV15, None, OP.mult)
+        ts(r("GM", 0, 128), r("ROWG", 0, 128), r("GF", 0, 1), None, OP.is_equal)
+        ts(r("IVD", 0, 128), ROWM, PF, VOID * 2048.0, OP.is_equal, OP.mult)
+        ts(r("I2K", 0, 128), ROWM, PF, 2048.0, OP.is_equal, OP.mult)
+        ts(r("PN", 0, 256), r("NF", 0, 256), -14680064.0, None, OP.add)
+        ts(r("I0", 0, 1), IF, 0.5, None, OP.is_lt)
+        ts(r("PADC", 0, 1), IF, 0.5, 4096.0, OP.is_gt, OP.mult)
+        tt(r("PADC", 0, 1), r("PADC", 0, 1), IF, OP.add)
+        ts(r("FM2", 0, 1), FM, -1.0, 2.0, OP.mult, OP.add)
+
+    def u_block(xb, b):
+        wsum(U0[b // 2] + (b % 2) * 64, "ZW", xb, 1024 * b, 1024, True, True)
+
+    def flip_copy(xb, first):
+        x0, full = r(xb, 0, P), r(xb, FO, FO + P)
+        dma("y", "sa", T.SG1[:], T[xb][15:128:16, 0:P], [r("SG1", 0, 256)], [x0])
+        dma("y", "xf", ap(full), T.x[:] if first else ap(x0), [full], [] if first else [x0])
+        ts(r("SG2", 0, 256), r("SG1", 0, 256), -1.0, 1.0, OP.mult, OP.add)
+        dma("y", "sb", T[xb][15:128:16, FO:FO + P], T.SG2[:], [full], [r("SG2", 0, 256)])
+
+    for b in range(4):
+        u_block("XB0", b)
+
+    ring = [0]
+
+    def pieces(n):
+        k = -(-n // BANK)
+        cut = [min(n, -(-n * i // (32 * k)) * 32) for i in range(k + 1)]
+        return list(zip(cut[:-1], cut[1:]))
+
+    for t in range(4):
+        X, X2 = "XB%d" % (t % 2), "XB%d" % (1 - t % 2)
+        xwin = r(X, 0, P)
+        tj = 1 + t % 3
+        TB = "T%d" % tj
+
+        def W(name, h, k=0):
+            return r(name, 256 * k, 256 * k + 256) if h == 2 else r(name, 256 * k + HC * h, 256 * k + HC * h + HC)
+
+        def kur(h, m):
+            return r("PS", KU0 + 256 * m, KU0 + 256 * m + 256) if h == 2 else r("PS", KU0 + 256 * m + HC * h, KU0 + 256 * m + HC * h + HC)
+
+        def list_ops(h):
+            cp(W("UR", h), r("PS", U0[h], U0[h] + HC))
+            ts(W("U", h), W("UR", h), 4095, None, OP.bitwise_and)
+            tt(W("US", h), W("U", h), W("U", h), OP.mult)
+            ts(kur(h, 0), W("U", h), r("KMF", 3 * t, 3 * t + 1), None, OP.mult)
+            ts(W("V1", h), W("US", h), 5, None, OP.arith_shift_right)
+            q_ops(h, 0)
+
+        def q_ops(h, m):
+            if m:
+                ts(kur(h, m), W("U", h), r("KMF", 3 * t + m, 3 * t + m + 1), None, OP.mult)
+            tt(W("QR", h, m), kur(h, m), W("V1", h), OP.add)
+            ts(W("QI", h, m), W("QR", h, m), 4095, None, OP.bitwise_and)
+            cp(W("QO", h, m), W("QI", h, m))
+
+        def q_more(m):
+            tt(W("EQ", 2, m), W("QI", 2, m), PIXW, OP.is_equal)
+            ts(W("QB", 2, m), W("QI", 2, m), 4096.0 * m - 16777216.0, None, OP.add)
+
+        def d_v(h, m):
+            oc, s = 256 * m + HC * h, SDT[3 * h + m]
+            tt(r("AD%d" % m, s, HALF), ind(xwin, r("QO", oc + s // 16, oc + HC)), r("NX", HALF * h + s, HALF * h + HALF), OP.subtract)
+
+        def d_s(h, m):
+            todo = []
+            for c, e in pieces(SDT[3 * h + m]):
+                k, n = ring[0] % 2, e - c
+                ring[0] += 1
+                oc = 256 * m + HC * h
+                act(r("XQ", 512 * k, 512 * k + n), ind(xwin, r("QO", oc + c // 16, oc + e // 16)), COPY)
+                mm(ps(6 + k, 0, n), r("IB", 0, 128), r("XQ", 512 * k, 512 * k + n), True, False)
+                mm(ps(6 + k, 0, n), r("IN", 0, 128), r(X, HALF * h + c, HALF * h + e), False, True)
+                todo.append((c, n, k))
+                if len(todo) > 1:
+                    d_abs(m, todo.pop(0))
+            return todo
+
+        def d_abs(m, job):
+            c, n, k = job
+            act(r("AD%d" % m, c, c + n), ps(6 + k, 0, n), ACT.Abs)
+
+        def d_vabs(h, m):
+            c = r("AD%d" % m, SDT[3 * h + m], HALF)
+            act(c, c, ACT.Abs)
+
+        def d_sum(h, m):
+            c = K0[h] + 128 * m
+            mm(r("PS", c, c + HC), r("IDF", 0, 128), W("QB", h, m), True, False)
+            mm(r("PS", c, c + HC), r("IEQ", 0, 128), W("EQ", h, m), False, False)
+            wsum(c, "ZD", "AD%d" % m, 0, HALF, False, True)
+
+        def choose(h):
+            c = K0[h]
+            cp(W("KA", h), r("PS", c, c + 128))
+            tt(W("KB", h), r("PS", c + 128, c + 256), W("KA", h), OP.min)
+            tt(W("KI", h), r("PS", c + 256, c + 384), W("KB", h), OP.min)
+            ts(W("IQ", h), W("KI", h), 4095, None, OP.bitwise_and)
+            cp(W("QSO", h), W("IQ", h))
+
+        def y_v(h, c0, c1):
+            c0, c1 = c0 + HALF * h, c1 + HALF * h
+            tt(r("YB", c0, c1), ind(xwin, r("QSO", c0 // 16, c1 // 16)), r("NX", c0, c1), OP.add)
+
+        def y_s(h):
+            c0 = HALF * h + SY[h]
+            act(r("YB", HALF * h, c0), ind(xwin, r("QSO", HC * h, c0 // 16)), COPY)
+
+        def y_sum(col, z, h):
+            wsum(col, z, "YB", HALF * h, HALF, True, False)
+            wsum(col, z, X, HALF * h, SY[h], False, True)
+
+        def h_ops(h):
+            tt(W("UQ", h), r("PS", UQ0[h], UQ0[h] + HC), W("U", h), OP.subtract)
+            ts(W("UA", h), W("UQ", h), 4095, None, OP.bitwise_and)
+            tt(W("UH", h), W("UA", h), W("U", h), OP.mult)
+            ts(W("IH", h), W("UH", h), 4, 4095, OP.arith_shift_right, OP.bitwise_and)
+            cp(W("HO", h), W("IH", h))
+
+        def t_v(h, c0, c1):
+            c0, c1 = c0 + HALF * h, c1 + HALF * h
+            tt(r("ZB", c0, c1), ind(r(TB, 0, P), r("HO", c0 // 16, c1 // 16)), r("YB", c0, c1), OP.subtract)
+
+        def t_s(h):
+            todo = []
+            for c, e in pieces(SET[h]):
+                k, n = ring[0] % 2, e - c
+                ring[0] += 1
+                p0 = HALF * h + c
+                act(r("NA", 512 * k, 512 * k + n), ind(r(TB, 0, P), r("HO", p0 // 16, (p0 + n) // 16)), COPY, scale=-1.0)
+                mm(ps(6 + k, 0, n), r("IB", 0, 128), r("YB", p0, p0 + n), True, False)
+                if c < SY[h]:
+                    n1 = min(n, SY[h] - c)
+                    mm(ps(6 + k, 0, n1), r("IB", 0, 128), r(X, p0, p0 + n1), False, False)
+                mm(ps(6 + k, 0, n), r("IB", 0, 128), r("NA", 512 * k, 512 * k + n), False, True)
+                todo.append((p0, n, k))
+                if len(todo) > 1:
+                    t_abs(todo.pop(0))
+            return todo
+
+        def t_abs(job):
+            p0, n, k = job
+            act(r("ZB", p0, p0 + n), ps(6 + k, 0, n), ACT.Abs)
+
+        def t_vabs(h, c0, c1):
+            act(r("ZB", HALF * h + c0, HALF * h + c1), r("ZB", HALF * h + c0, HALF * h + c1), ACT.Abs)
+
+        def e_sum(h, c0, c1):
+            w0, w1 = HC * h + c0 // 16, HC * h + c1 // 16
+            o = r("PS", KEY + w0, KEY + w1)
+            mm(o, r("IDF", 0, 128), r("PN", w0, w1), True, False)
+            mm(o, r("I2K", 0, 128), r("KF", w0, w1), False, False)
+            mm(o, r("IVD", 0, 128), r("VD", w0, w1), False, False)
+            wsum(KEY + w0, "ZE", "ZB", HALF * h + c0, c1 - c0, False, True)
+
+        if t:
+            for h in (0, 1):
+                act(r("NX", NXC[h], HALF * h + HALF), r(X, NXC[h], HALF * h + HALF), COPY)
+        list_ops(0)
+        pend = None
+        for n, (h, m) in enumerate([(h, m) for h in (0, 1) for m in (0, 1, 2)]):
+            left = d_s(h, m)
+            if pend is not None:
+                d_vabs(*pend)
+            for job in left:
+                d_abs(m, job)
+            if n == 1:
+                q_more(0)
+                q_more(1)
+            elif n == 2:
+                q_more(2)
+            if pend is not None:
+                d_sum(*pend)
+            pend = (h, m)
+            if n == 0:
+                d_v(0, 0)
+                list_ops(1)
+                q_ops(2, 1)
+                d_v(0, 1)
+                q_ops(2, 2)
+            elif n == 1:
+                d_v(0, 2)
+            elif n == 2:
+                if t == 0:
+                    late_constants()
+            else:
+                d_v(h, m)
+                if n == 3:
+                    flip_copy(X, t == 0)
+                if n == 4:
+                    choose(0)
+        d_vabs(1, 2)
+        d_sum(1, 2)
+        y_s(0)
+        y_v(0, SY[0], HALF)
+        y_sum(UQ0[0], "ZW", 0)
+        y_sum(SG0, "ZS", 0)
+        choose(1)
+        y_s(1)
+        y_v(1, SY[1], YC)
+        for (j, tu) in UPD:
+            if j == tj and tu < t:
+                RU = "RU%d%d" % (j, tu)
+                cp(r("OFF", 8 + 2 * tu, 9 + 2 * tu), r(RU, 16, 17))
+                cp(ind(r(TB, 0, P + 16), r("OFF", 8 + 2 * tu, 9 + 2 * tu)), r(RU, 0, 16))
+        h_ops(0)
+        y_v(1, YC, HALF)
+        mid = (SET[0] + HALF) // 2 // 32 * 32
+        left = t_s(0)
+        y_sum(UQ0[1], "ZW", 1)
+        y_sum(SG0 + HC, "ZS", 1)
+        ts(W("KD", 2), W("KI", 2), 14, None, OP.arith_shift_right)
+        t_v(0, SET[0], mid)
+        cp(W("KF", 2), W("KD", 2))
+        ts(W("VD", 2), W("KD", 2), VOID - 1024.0, None, OP.is_ge)
+        h_ops(1)
+        t_v(0, mid, HALF)
+        for job in left:
+            t_abs(job)
+        t_vabs(0, SET[0], mid)
+        left = t_s(1)
+        t_vabs(0, mid, HALF)
+        e_sum(0, 0, HALF)
+        for job in left:
+            t_abs(job)
+        cuts = [SET[1], CUT[0], CUT[1], HALF]
+        for c0, c1 in zip(cuts[:-1], cuts[1:]):
+            t_v(1, c0, c1)
+            t_vabs(1, c0, c1)
+        e_sum(1, 0, CUT[0])
+        e_sum(1, CUT[0], HALF)
+        red(cf(0), r("PS", KEY, KEY + HC))
+        ts(r("R32", 0, 16), r("D16", 0, 16), cf(0), None, OP.mult)
+        tt(ps(2, 0, 256), W("IQ", 2), PIXW, OP.min)
+        ts(W("DIRT", 2), r("PS", SG0, SG0 + 256), 1.0, None, OP.not_equal)
+        tt(W("CC", 2), ps(2, 0, 256), W("DIRT", 2), OP.mult)
+        red(cf(1), r("PS", KEY + HC, KEY + 2 * HC))
+        ts(r("R32", 16, 32), r("D16", 0, 16), cf(1), None, OP.mult)
+
+        s1, s2 = SMALL1, SMALL2
+        mm(r("PS", s1, s1 + 32), r("GM", 0, 128), r("R32", 0, 32), True, True)
+        kk = r("CI", 0, 1)
+        red(kk, r("PS", s1, s1 + 32))
+        ts(r("CI", 1, 2), kk, 4, 255, OP.arith_shift_right, OP.bitwise_and)
+        ts(r("CI", 2, 3), kk, 15, None, OP.bitwise_and)
+        cp(r("OFF", 0, 1), r("CI", 1, 2))
+        tt(cf(2), r("II", 0, 1), r("CI", 2, 3), OP.is_equal)
+        ts(r("CI", 3, 4), kk, 4095, None, OP.bitwise_and)
+        for n, w in enumerate(["IQ", "DIRT", "IH"]):
+            ts(r("GQ", 16 * n, 16 * n + 16), ind(r(w, 0, 256), r("OFF", 0, 1)), cf(2), None, OP.mult)
+        mm(r("PS", s2, s2 + 48), r("GM", 0, 128), r("GQ", 0, 48), True, True)
+        cp(cf(3), r("CI", 3, 4))
+        q1, dirc, hc = r("PS", s2, s2 + 1), r("PS", s2 + 16, s2 + 17), r("PS", s2 + 32, s2 + 33)
+        a, b = cf(6), cf(7)
+        ts(cf(4), q1, cf(3), 0.5, OP.min, OP.add)
+        ts(cf(5), q1, cf(3), -0.5, OP.max, OP.add)
+        ts(CLAMP, r("CC", 0, 256), cf(4), cf(5), OP.max, OP.min)
+        ts(a, q1, cf(3), None, OP.min)
+        ts(b, q1, cf(3), None, OP.max)
+        tt(r("NN", 0, 256), CLAMP, r("CC", 0, 256), OP.is_equal)
+        ts(r("OFF", 2, 3), q1, cf(3), None, OP.min)
+        ts(r("OFF", 4, 5), q1, cf(3), None, OP.max)
+        tt(r("K2", 0, 256), r("PS", KEY, KEY + 256), r("NN", 0, 256), OP.mult)
+        if t < 3:
+            ts(r("UP%d" % t, 16, 17), hc, r("I0", 0, 1), r("PADC", 0, 1), OP.mult, OP.add)
+        cp(cf(8), dirc)
+        red(cf(0), r("K2", 0, 256))
+        act(cf(9), cf(8), COPY, scale=-1.0, bias=1.0)
+        act(cf(10), a, COPY, bias=b)
+        act(cf(18), cf(9), COPY, scale=FO + 1.0)
+        act(cf(12), a, COPY, scale=-1.0, bias=b)
+        act(cf(11), cf(10), COPY, scale=cf(9), bias=cf(18))
+        act(cf(32), cf(12), COPY, scale=cf(8))
+        act(cf(19), cf(11), COPY, scale=-1.0)
+        act(cf(13), cf(12), COPY, scale=cf(8), bias=cf(19))
+        act(cf(20), cf(9), COPY, scale=4095.0)
+        act(cf(21), b, COPY, scale=cf(8), bias=cf(20))
+        act(cf(25), cf(32), COPY, scale=-1.0)
+        act(r("XA", 0, 16), ind(xwin, r("OFF", 2, 3)), COPY, scale=r("FM2", 0, 1))
+        act(r("XC", 0, 16), ind(xwin, r("OFF", 4, 5)), COPY, scale=FM)
+        ts(r("R32", 0, 16), r("D16", 0, 16), cf(0), None, OP.mult)
+        mm(r("PS", s1, s1 + 16), r("GM", 0, 128), r("R32", 0, 16), True, True)
+        ts(r("OFF", 6, 7), a, r("I0", 0, 1), r("PADC", 0, 1), OP.mult, OP.add)
+        kk = r("CI", 4, 5)
+        red(kk, r("PS", s1, s1 + 16))
+        ts(r("CI", 5, 6), kk, 4, 255, OP.arith_shift_right, OP.bitwise_and)
+        ts(r("CI", 6, 7), kk, 15, None, OP.bitwise_and)
+        cp(r("OFF", 0, 1), r("CI", 5, 6))
+        tt(cf(33), r("II", 0, 1), r("CI", 6, 7), OP.is_equal)
+        ts(r("CI", 7, 8), kk, 4095, None, OP.bitwise_and)
+        ts(r("GQ", 48, 64), ind(r("IQ", 0, 256), r("OFF", 0, 1)), cf(33), None, OP.mult)
+        mm(r("PS", s2, s2 + 16), r("GM", 0, 128), r("GQ", 48, 64), True, True)
+        ts(cf(15), kk, 0.0, cf(8), OP.is_lt, OP.mult)
+        ts(r("Y0", 0, 256), r("NF", 0, 256), a, cf(13), OP.is_gt, OP.mult)
+        mm(YSUM, r("IDF", 0, 128), r("NF", 0, 256), True, False)
+        mm(YSUM, r("IDF", 0, 128), r("Y0", 0, 256), False, False)
+        cp(cf(14), r("CI", 7, 8))
+        ts(cf(16), cf(15), -8192.0, 8192.0, OP.mult, OP.add)
+        tt(r("NI", 0, 16), r("XA", 0, 16), r("XC", 0, 16), OP.add)
+        tt(cf(17), cf(16), b, OP.add)
+        ts(r("Y1", 0, 256), r("NF", 0, 256), b, cf(11), OP.is_gt, OP.mult)
+        mm(YSUM, r("IDF", 0, 128), r("Y1", 0, 256), False, True)
+        act(r("VA", 0, 256), YSUM, ACT.Abs)
+        q2 = r("PS", s2, s2 + 1)
+        d, L = cf(27), cf(28)
+        ts(cf(22), q2, cf(14), cf(17), OP.max, OP.is_gt)
+        ts(cf(23), q2, cf(14), cf(21), OP.min, OP.subtract)
+        ts(cf(24), q2, cf(14), 4095.0, OP.max, OP.subtract)
+        ts(cf(26), cf(23), cf(22), cf(21), OP.mult, OP.add)
+        ts(d, cf(24), cf(22), 4095.0, OP.mult, OP.add)
+        ts(r("NJ", 0, 16), r("NI", 0, 16), 1, None, OP.arith_shift_right)
+        tt(L, d, cf(26), OP.subtract)
+        act(cf(29), cf(12), COPY, scale=-1.0, bias=d)
+        act(cf(31), L, COPY, bias=a)
+        act(cf(30), L, COPY, scale=-1.0)
+        cp(ind(r(X, 0, P + 16), r("OFF", 6, 7)), r("NJ", 0, 16))
+
+        def order(h):
+            o = ps(6 + h, 0, HC)
+            ts(W("TC", h), W("NF", h), d, L, OP.is_gt, OP.mult)
+            ts(W("TB", h), W("NF", h), cf(31), cf(25), OP.is_gt, OP.mult)
+            ts(W("TA", h), W("NF", h), cf(29), cf(30), OP.is_gt, OP.mult)
+            mm(o, r("IDF", 0, 128), W("VA", h), True, False)
+            mm(o, r("IDF", 0, 128), W("TC", h), False, False)
+            mm(o, r("IDF", 0, 128), W("TB", h), False, False)
+            mm(o, r("IDF", 0, 128), W("TA", h), False, True)
+
+        def move_s(c0, c1):
+            act(r(X2, c0, c1), ind(r(X, 0, XW), r("RO", c0 // 16, c1 // 16)), COPY)
+
+        def move_v(c0, c1):
+            cp(r(X2, c0, c1), ind(r(X, 0, XW), r("RO", c0 // 16, c1 // 16)))
+
+        order(0)
+        order(1)
+        cp(W("RO", 0), ps(6, 0, HC))
+        cp(W("RO", 1), ps(7, 0, HC))
+        cuts = [(0, 1024, "s"), (RS, 3072, "v"), (1024, 2048, "s"), (3072, P, "v"), (2048, RS, "s")]
+        for n, (c0, c1, q) in enumerate(cuts):
+            (move_s if q == "s" else move_v)(c0, c1)
+            if t == 3:
+                dma("y", "y%d" % n, T.y[:, c0:c1], T[X2][:, c0:c1], [], [r(X2, c0, c1)])
+        if t < 3:
+            for bl in range(4):
+                u_block(X2, bl)
+            ts(r("UP%d" % t, 0, 16), r("NJ", 0, 16), 2.0, None, OP.mult)
+            for (j, tu) in UPD:
+                if tu == t:
+                    send(asker[j], T["RU%d%d" % (j, t)][:], r("UP%d" % t, 0, 32), "ru%d%d" % (j, t), lanes(core, asker[j]))
+
+    total["ls"] = sent[0]
+    for sem, val in total.items():
+        if clock["g"].get(sem, 0) < val:
+            g.wait_ge(T.sem[sem], val)

@@ -6,12 +6,12 @@ XW = FO + P
 HALF = 2048
 HC = 128
 BANK = 512
-SDT = (1856, 672, 480, 384, 384, 512)
-SY = (576, 448)
+SDT = (1856, 672, 480, 352, 512, 512)
+SY = (608, 448)
 SET = (768, 448)
-YC = 1024
-CUT = (1024, 1472)
-RS = 2432
+YC = 1248
+CUT = (1024, 1536)
+MOVE = ((0, 1024, "s"), (1024, 2048, "v"), (2048, 3072, "s"), (3072, 4096, "v"))
 VOID = 1920.0
 
 BF, F4, I4, U2 = "bfloat16", "float32", "int32", "uint16"
@@ -32,7 +32,7 @@ for _names, _w, _d in ((("XB0", "XB1"), XW, BF), (("T1", "T2", "T3"), P + 16, BF
         SCRATCH[_n] = ("sbuf", [128, _w], _d)
 UPD = [(1, 0), (2, 0), (3, 0), (1, 1), (3, 1), (1, 2)]
 SEMAPHORES = (["cv", "cs", "cp", "cg", "km", "wt", "xf", "sa", "sb", "ls"] + ["x%d" % i for i in range(4)] + ["tm%d" % i for i in range(2)]
-              + ["nx0", "nx1"] + ["y%d" % i for i in range(6)] + ["rt1", "rt2", "rt3"] + ["ru%d%d" % u for u in UPD])
+              + ["nx0", "nx1"] + ["y%d" % i for i in range(4)] + ["rt1", "rt2", "rt3"] + ["ru%d%d" % u for u in UPD])
 
 OP = AluOpType
 ACT = ActivationFunctionType
@@ -298,6 +298,11 @@ def rank_program(g, core, T, topo):
         cut = [min(n, -(-n * i // (32 * k)) * 32) for i in range(k + 1)]
         return list(zip(cut[:-1], cut[1:]))
 
+    def run(*chains):
+        chains = list(chains)
+        while chains:
+            chains = [c for c in chains if next(c, 0) is None]
+
     for t in range(4):
         X, X2 = "XB%d" % (t % 2), "XB%d" % (1 - t % 2)
         xwin = r(X, 0, P)
@@ -308,21 +313,28 @@ def rank_program(g, core, T, topo):
             return r(name, 256 * k, 256 * k + 256) if h == 2 else r(name, 256 * k + HC * h, 256 * k + HC * h + HC)
 
         def kur(h, m):
-            return r("PS", KU0 + 256 * m, KU0 + 256 * m + 256) if h == 2 else r("PS", KU0 + 256 * m + HC * h, KU0 + 256 * m + HC * h + HC)
+            return r("PS", KU0 + 256 * m + HC * h, KU0 + 256 * m + HC * h + HC)
 
         def list_ops(h):
             cp(W("UR", h), r("PS", U0[h], U0[h] + HC))
+            yield
             ts(W("U", h), W("UR", h), 4095, None, OP.bitwise_and)
+            yield
             tt(W("US", h), W("U", h), W("U", h), OP.mult)
             ts(kur(h, 0), W("U", h), r("KMF", 3 * t, 3 * t + 1), None, OP.mult)
             ts(W("V1", h), W("US", h), 5, None, OP.arith_shift_right)
-            q_ops(h, 0)
+            yield
+            for _ in q_ops(h, 0):
+                yield
 
         def q_ops(h, m):
             if m:
                 ts(kur(h, m), W("U", h), r("KMF", 3 * t + m, 3 * t + m + 1), None, OP.mult)
+                yield
             tt(W("QR", h, m), kur(h, m), W("V1", h), OP.add)
+            yield
             ts(W("QI", h, m), W("QR", h, m), 4095, None, OP.bitwise_and)
+            yield
             cp(W("QO", h, m), W("QI", h, m))
 
         def q_more(m):
@@ -377,12 +389,17 @@ def rank_program(g, core, T, topo):
             c0 = HALF * h + SY[h]
             act(r("YB", HALF * h, c0), ind(xwin, r("QSO", HC * h, c0 // 16)), COPY)
 
-        def y_sum(col, z, h):
-            wsum(col, z, "YB", HALF * h, HALF, True, False)
-            wsum(col, z, X, HALF * h, SY[h], False, True)
+        def u_sum(h):
+            wsum(UQ0[h], "ZW", "YB", HALF * h, HALF, True, True)
+
+        def s_sum(h):
+            wsum(SG0 + HC * h, "ZS", "YB", HALF * h, HALF, True, False)
+            wsum(SG0 + HC * h, "ZS", X, HALF * h, SY[h], False, True)
 
         def h_ops(h):
-            tt(W("UQ", h), r("PS", UQ0[h], UQ0[h] + HC), W("U", h), OP.subtract)
+            s, c = SY[h] // 16, HC * h
+            cp(r("UQ", c, c + s), r("PS", UQ0[h], UQ0[h] + s))
+            tt(r("UQ", c + s, c + HC), r("PS", UQ0[h] + s, UQ0[h] + HC), r("U", c + s, c + HC), OP.subtract)
             ts(W("UA", h), W("UQ", h), 4095, None, OP.bitwise_and)
             tt(W("UH", h), W("UA", h), W("U", h), OP.mult)
             ts(W("IH", h), W("UH", h), 4, 4095, OP.arith_shift_right, OP.bitwise_and)
@@ -416,18 +433,21 @@ def rank_program(g, core, T, topo):
         def t_vabs(h, c0, c1):
             act(r("ZB", HALF * h + c0, HALF * h + c1), r("ZB", HALF * h + c0, HALF * h + c1), ACT.Abs)
 
-        def e_sum(h, c0, c1):
-            w0, w1 = HC * h + c0 // 16, HC * h + c1 // 16
+        def e_head(h):
+            w0, w1 = HC * h, HC * h + HC
             o = r("PS", KEY + w0, KEY + w1)
             mm(o, r("IDF", 0, 128), r("PN", w0, w1), True, False)
             mm(o, r("I2K", 0, 128), r("KF", w0, w1), False, False)
             mm(o, r("IVD", 0, 128), r("VD", w0, w1), False, False)
-            wsum(KEY + w0, "ZE", "ZB", HALF * h + c0, c1 - c0, False, True)
+
+        def e_sum(h, c0, c1):
+            wsum(KEY + HC * h + c0 // 16, "ZE", "ZB", HALF * h + c0, c1 - c0, False, c1 == HALF)
 
         if t:
-            for h in (0, 1):
-                act(r("NX", NXC[h], HALF * h + HALF), r(X, NXC[h], HALF * h + HALF), COPY)
-        list_ops(0)
+            act(r("NX", NXC[0], HALF), r(X, NXC[0], HALF), COPY)
+            c = r("NX", NXC[1], P)
+            dma("y", "nx1", ap(c), T[X][:, NXC[1]:P], [c], [r(X, NXC[1], P)])
+        run(list_ops(0))
         pend = None
         for n, (h, m) in enumerate([(h, m) for h in (0, 1) for m in (0, 1, 2)]):
             left = d_s(h, m)
@@ -445,10 +465,9 @@ def rank_program(g, core, T, topo):
             pend = (h, m)
             if n == 0:
                 d_v(0, 0)
-                list_ops(1)
-                q_ops(2, 1)
+                run(list_ops(1), q_ops(0, 1))
                 d_v(0, 1)
-                q_ops(2, 2)
+                run(q_ops(0, 2), q_ops(1, 1), q_ops(1, 2))
             elif n == 1:
                 d_v(0, 2)
             elif n == 2:
@@ -464,8 +483,8 @@ def rank_program(g, core, T, topo):
         d_sum(1, 2)
         y_s(0)
         y_v(0, SY[0], HALF)
-        y_sum(UQ0[0], "ZW", 0)
-        y_sum(SG0, "ZS", 0)
+        u_sum(0)
+        s_sum(0)
         choose(1)
         y_s(1)
         y_v(1, SY[1], YC)
@@ -478,14 +497,16 @@ def rank_program(g, core, T, topo):
         y_v(1, YC, HALF)
         mid = (SET[0] + HALF) // 2 // 32 * 32
         left = t_s(0)
-        y_sum(UQ0[1], "ZW", 1)
-        y_sum(SG0 + HC, "ZS", 1)
+        u_sum(1)
         ts(W("KD", 2), W("KI", 2), 14, None, OP.arith_shift_right)
         t_v(0, SET[0], mid)
         cp(W("KF", 2), W("KD", 2))
         ts(W("VD", 2), W("KD", 2), VOID - 1024.0, None, OP.is_ge)
+        e_head(0)
+        e_head(1)
         h_ops(1)
         t_v(0, mid, HALF)
+        s_sum(1)
         for job in left:
             t_abs(job)
         t_vabs(0, SET[0], mid)
@@ -535,6 +556,7 @@ def rank_program(g, core, T, topo):
         if t < 3:
             ts(r("UP%d" % t, 16, 17), hc, r("I0", 0, 1), r("PADC", 0, 1), OP.mult, OP.add)
         cp(cf(8), dirc)
+        mm(YSUM, r("IDF", 0, 128), r("NF", 0, 256), True, False)
         red(cf(0), r("K2", 0, 256))
         act(cf(9), cf(8), COPY, scale=-1.0, bias=1.0)
         act(cf(10), a, COPY, bias=b)
@@ -563,7 +585,6 @@ def rank_program(g, core, T, topo):
         mm(r("PS", s2, s2 + 16), r("GM", 0, 128), r("GQ", 48, 64), True, True)
         ts(cf(15), kk, 0.0, cf(8), OP.is_lt, OP.mult)
         ts(r("Y0", 0, 256), r("NF", 0, 256), a, cf(13), OP.is_gt, OP.mult)
-        mm(YSUM, r("IDF", 0, 128), r("NF", 0, 256), True, False)
         mm(YSUM, r("IDF", 0, 128), r("Y0", 0, 256), False, False)
         cp(cf(14), r("CI", 7, 8))
         ts(cf(16), cf(15), -8192.0, 8192.0, OP.mult, OP.add)
@@ -581,34 +602,32 @@ def rank_program(g, core, T, topo):
         ts(d, cf(24), cf(22), 4095.0, OP.mult, OP.add)
         ts(r("NJ", 0, 16), r("NI", 0, 16), 1, None, OP.arith_shift_right)
         tt(L, d, cf(26), OP.subtract)
-        act(cf(29), cf(12), COPY, scale=-1.0, bias=d)
-        act(cf(31), L, COPY, bias=a)
-        act(cf(30), L, COPY, scale=-1.0)
+        tt(cf(29), d, cf(12), OP.subtract)
         cp(ind(r(X, 0, P + 16), r("OFF", 6, 7)), r("NJ", 0, 16))
+        tt(cf(31), L, a, OP.add)
+        ts(cf(30), L, -1.0, None, OP.mult)
 
-        def order(h):
-            o = ps(6 + h, 0, HC)
-            ts(W("TC", h), W("NF", h), d, L, OP.is_gt, OP.mult)
+        o1, o2 = [[ps(4 + k, HC * h, HC * h + HC) for h in (0, 1)] for k in (0, 1)]
+        o3 = [r("PS", K0[h], K0[h] + HC) for h in (0, 1)]
+        both = (0, 1)
+        for h in both:
+            ts(o1[h], W("NF", h), d, L, OP.is_gt, OP.mult)
             ts(W("TB", h), W("NF", h), cf(31), cf(25), OP.is_gt, OP.mult)
-            ts(W("TA", h), W("NF", h), cf(29), cf(30), OP.is_gt, OP.mult)
-            mm(o, r("IDF", 0, 128), W("VA", h), True, False)
-            mm(o, r("IDF", 0, 128), W("TC", h), False, False)
-            mm(o, r("IDF", 0, 128), W("TB", h), False, False)
-            mm(o, r("IDF", 0, 128), W("TA", h), False, True)
-
-        def move_s(c0, c1):
-            act(r(X2, c0, c1), ind(r(X, 0, XW), r("RO", c0 // 16, c1 // 16)), COPY)
-
-        def move_v(c0, c1):
-            cp(r(X2, c0, c1), ind(r(X, 0, XW), r("RO", c0 // 16, c1 // 16)))
-
-        order(0)
-        order(1)
-        cp(W("RO", 0), ps(6, 0, HC))
-        cp(W("RO", 1), ps(7, 0, HC))
-        cuts = [(0, 1024, "s"), (RS, 3072, "v"), (1024, 2048, "s"), (3072, P, "v"), (2048, RS, "s")]
-        for n, (c0, c1, q) in enumerate(cuts):
-            (move_s if q == "s" else move_v)(c0, c1)
+        for h in both:
+            ts(o2[h], W("NF", h), cf(29), cf(30), OP.is_gt, OP.mult)
+            tt(W("TA", h), o1[h], W("TB", h), OP.add)
+        for h in both:
+            tt(o3[h], o2[h], W("TA", h), OP.add)
+        for h in both:
+            tt(W("TC", h), o3[h], W("VA", h), OP.add)
+        for h in both:
+            cp(W("RO", h), W("TC", h))
+        for n, (c0, c1, q) in enumerate(MOVE):
+            src = ind(r(X, 0, XW), r("RO", c0 // 16, c1 // 16))
+            if q == "s":
+                act(r(X2, c0, c1), src, COPY)
+            else:
+                cp(r(X2, c0, c1), src)
             if t == 3:
                 dma("y", "y%d" % n, T.y[:, c0:c1], T[X2][:, c0:c1], [], [r(X2, c0, c1)])
         if t < 3:

from concourse.mybir import AluOpType, AxisListType, ActivationFunctionType

P = 4096
FO = P + 16
XW = FO + P
HALF = 2048
HC = 128
BANK = 512
SDT = (1856, 672, 480, 352, 512, 512)
SY = (608, 448)
SET = (768, 448)
YC = 1248
CUT = (1024, 1536)
MOVE = ((0, 1024, "s"), (1024, 2048, "v"), (2048, 3072, "s"), (3072, 4096, "v"))
VOID = 1920.0

BF, F4, I4, U2 = "bfloat16", "float32", "int32", "uint16"
SCRATCH = {"PS": ("psum", [128, 4096], F4)}
for _names, _w, _d in ((("XB0", "XB1"), XW, BF), (("T1", "T2", "T3"), P + 16, BF), (("TMB", "YB", "ZB", "NX"), P, BF),
                       (("AD0", "AD1", "AD2"), HALF, BF), (("XQ", "NA"), 1024, BF), (("SG1", "SG2", "VD"), 256, BF), (("EQ",), 768, BF),
                       (("KM",), 12, I4), (("WT", "PIX", "II", "GI"), 1, I4), (("KMF",), 12, F4),
                       (("WTF", "IF", "GF", "PF", "G15", "FM", "FM2", "SM", "I0", "PADC"), 1, F4),
                       (("ROW", "Z0"), 144, F4), (("ROWI", "ROWG"), 128, I4), (("NB", "NF", "PN"), 256, F4),
                       (("GM", "IDF", "I2K"), 128, F4), (("D16",), 16, F4), (("ZW", "ZD", "ZE", "ZS"), 144, BF),
                       (("IB", "IN", "IEQ", "IVD"), 128, BF), (("UR", "U", "US", "V1", "KI", "IQ", "IH", "KD", "UQ", "UA", "UH"), 256, I4),
                       (("QR", "QI"), 768, I4), (("QO",), 768, U2), (("QB",), 768, F4), (("QSO", "HO", "RO"), 256, U2),
                       (("KA", "KB", "KF", "DIRT", "CC", "NN", "K2", "Y0", "Y1", "VA", "TA", "TB", "TC"), 256, F4),
                       (("CF",), 64, F4), (("CI",), 16, I4), (("OFF",), 16, U2), (("R32",), 32, F4), (("GQ",), 64, F4),
                       (("XA", "XC"), 16, F4), (("NI", "NJ"), 16, I4),
                       (("UP0", "UP1", "UP2", "RU10", "RU11", "RU12", "RU20", "RU30", "RU31"), 32, F4)):
    for _n in _names:
        SCRATCH[_n] = ("sbuf", [128, _w], _d)
UPD = [(1, 0), (2, 0), (3, 0), (1, 1), (3, 1), (1, 2)]
SEMAPHORES = (["cv", "cs", "cp", "cg", "km", "wt", "xf", "sa", "sb", "ls"] + ["x%d" % i for i in range(4)] + ["tm%d" % i for i in range(2)]
              + ["nx0", "nx1"] + ["y%d" % i for i in range(4)] + ["rt1", "rt2", "rt3"] + ["ru%d%d" % u for u in UPD])

OP = AluOpType
ACT = ActivationFunctionType
COPY = ACT.Identity


def r(name, c0, c1, step=1):
    return ("r", name, c0, c1, step)


def ind(win, off):
    return ("i", win, off)


def rank_program(g, core, T, topo):
    rank = T.rank_of(core)
    if rank is None:
        return
    N = len(T.cores)
    queue = {"v": g.vector, "s": g.scalar, "p": g.tensor, "g": g, "y": g.sync}
    own = {"v": "cv", "s": "cs", "p": "cp", "g": "cg"}
    total = {}
    clock = {q: {} for q in queue}
    rec = {}
    bank = {}
    serial = [0]

    def merge(a, b):
        for k, v in b.items():
            if a.get(k, 0) < v:
                a[k] = v

    def need(q, outs, ins):
        deps = []
        for (_, name, c0, c1, st) in ins:
            for x in rec.get(name, []):
                if x[2] and x[0] < c1 and c0 < x[1]:
                    deps.append(x)
        for (_, name, c0, c1, st) in outs:
            for x in rec.get(name, []):
                if x[0] < c1 and c0 < x[1] and not (x[3] == q and q == "p"):
                    deps.append(x)
        for (_, name, c0, c1, st) in list(outs) + list(ins):
            if name == "PS":
                for b in range(c0 // BANK, (c1 - 1) // BANK + 1):
                    for q2, x in bank.get(b, {}).items():
                        if q2 != q:
                            deps.append(x)
        ck = clock[q]
        deps.sort(key=lambda x: -x[6])
        todo = {}
        for x in deps:
            sem, val = x[4]
            if ck.get(sem, 0) < val:
                todo[sem] = max(todo.get(sem, 0), val)
                merge(ck, x[5])
        for sem, val in todo.items():
            queue[q].wait_ge(T.sem[sem], val)

    def note(q, ck, outs, ins, tok):
        serial[0] += 1
        snap = dict(ck)
        merge(snap, {tok[0]: tok[1]})
        for lst, w in ((ins, False), (outs, True)):
            for (_, name, c0, c1, st) in lst:
                new = (c0, c1, w, q, tok, snap, serial[0])
                old = rec.get(name, [])
                if w and st == 1:
                    old = [x for x in old if not (c0 <= x[0] and x[1] <= c1)]
                elif not w:
                    old = [x for x in old if x[2] or x[3] != q or not (c0 <= x[0] and x[1] <= c1)]
                old.append(new)
                rec[name] = old
                if name == "PS":
                    for b in range(c0 // BANK, (c1 - 1) // BANK + 1):
                        bank.setdefault(b, {})[q] = new

    def ap(a):
        if isinstance(a, tuple) and a and a[0] == "r":
            return T[a[1]][:, a[2]:a[3]] if a[4] == 1 else T[a[1]][:, a[2]:a[3]:a[4]]
        if isinstance(a, tuple) and a and a[0] == "i":
            return ap(a[1]).indirect(ap(a[2]))
        return a

    def regs(a):
        if isinstance(a, tuple) and a and a[0] == "r":
            return [a]
        if isinstance(a, tuple) and a and a[0] == "i":
            return [a[1], a[2]]
        return []

    def bump(sem, n):
        total[sem] = total.get(sem, 0) + n
        return (sem, total[sem])

    def E(q, call, out, *args, **kw):
        outs = regs(out)
        ins = outs[1:]
        outs = outs[:1]
        for a in list(args) + list(kw.values()):
            ins = ins + regs(a)
        need(q, outs, ins)
        tok = bump(own[q], 1)
        call(ap(out), *[ap(a) for a in args], **{k: ap(v) for k, v in kw.items()}).then_inc(T.sem[tok[0]], 1)
        note(q, clock[q], outs, ins, tok)

    def dma(q, sem, out_ap, in_ap, outs, ins):
        need(q, outs, ins)
        tok = bump(sem, 16)
        queue[q].dma_start(out_ap, in_ap).then_inc(T.sem[sem], 16)
        note(q + "dma", clock[q], outs, ins, tok)

    def arrival(outs, tok):
        note("remote", {}, outs, [], tok)

    def ts(out, a, s1, s2, o0, o1=None):
        if o1 is None:
            E("v", g.vector.tensor_scalar, out, a, s1, None, o0)
        else:
            E("v", g.vector.tensor_scalar, out, a, s1, s2, o0, o1)

    def tt(out, a, b, o):
        E("v", g.vector.tensor_tensor, out, a, b, o)

    def cp(out, a):
        E("v", g.vector.tensor_copy, out, a)

    def red(out, a):
        E("v", g.vector.tensor_reduce, out, a, AxisListType.X, OP.min)

    def act(out, a, f, **kw):
        E("s", g.scalar.activation, out, a, f, **kw)

    def mm(out, lhsT, rhs, start, stop):
        E("p", g.tensor.matmul, out, lhsT, rhs, start, stop)

    def ps(b, c0, c1):
        return r("PS", b * BANK + c0, b * BANK + c1)

    def cf(k):
        return r("CF", k, k + 1)

    def wsum(col, z, buf, c0, n, start, stop):
        for i in range(16):
            mm(r("PS", col, col + n // 16), r(z, 15 - i, 143 - i), r(buf, c0 + i, c0 + n, 16), start and i == 0, stop and i == 15)

    U0, UQ0, SG0, PIX0 = (0, BANK + 128), (128, BANK + 256), 384, 2 * BANK + 384
    K0 = (2 * BANK, 3 * BANK + 128)
    KU0, KEY = 4 * BANK, 4 * BANK + 384
    SMALL1, SMALL2 = 256, BANK + 384
    CLAMP, YSUM = ps(7, 0, 256), ps(6, 256, 512)
    PIXW = r("PS", PIX0, PIX0 + 256)

    dma("s", "wt", T.WT[:], T.wt[:], [r("WT", 0, 1)], [])
    dma("s", "km", T.KM[:], T.km[:], [r("KM", 0, 12)], [])
    for i in range(4):
        c = r("XB0", 1024 * i, 1024 * i + 1024)
        dma("y", "x%d" % i, ap(c), T.x[:, 1024 * i:1024 * i + 1024], [c], [])
    for i in range(2):
        c = r("TMB", 2048 * i, 2048 * i + 2048)
        dma("s", "tm%d" % i, ap(c), T.tm[:, 2048 * i:2048 * i + 2048], [c], [])
    NXC = [HALF * h + min(SDT[3 * h:3 * h + 3] + SY[h:h + 1]) for h in (0, 1)]
    for h in (0, 1):
        c = r("NX", NXC[h], HALF * h + HALF)
        dma("y", "nx%d" % h, ap(c), T.x[:, NXC[h]:HALF * h + HALF], [c], [])
    E("g", g.iota, r("PIX", 0, 1), [[0, 1]], 0, 1)
    E("g", g.iota, r("ROW", 0, 144), [[1, 144]], 0, 0, allow_small_or_imprecise_dtypes=True)
    E("g", g.iota, r("NB", 0, 256), [[16, 256]], 0, 0, allow_small_or_imprecise_dtypes=True)
    E("g", g.iota, r("ROWI", 0, 128), [[1, 128]], 0, 0)
    for j in (1, 2, 3):
        E("v", g.vector.memset, r("T%d" % j, P, P + 16), 0.0)
    for j in (0, 1):
        E("v", g.vector.memset, r("XB%d" % j, P, P + 16), 0.0)
    for j in (0, 1, 2):
        E("v", g.vector.memset, r("UP%d" % j, 0, 32), 0.0)
    IF, PF, FM, INV15 = r("IF", 0, 1), r("PF", 0, 1), r("FM", 0, 1), r("SM", 0, 1)
    Z0, ROWM = r("Z0", 0, 144), r("ROW", 0, 128)
    ts(r("II", 0, 1), r("PIX", 0, 1), 15, None, OP.bitwise_and)
    ts(r("GI", 0, 1), r("PIX", 0, 1), 4, None, OP.arith_shift_right)
    cp(PF, r("PIX", 0, 1))
    cp(IF, r("II", 0, 1))
    cp(r("GF", 0, 1), r("GI", 0, 1))
    cp(r("WTF", 0, 1), r("WT", 0, 1))
    ts(r("G15", 0, 1), r("GF", 0, 1), 16.0, 15.0, OP.mult, OP.add)
    ts(FM, IF, 14.5, None, OP.is_lt)
    ts(INV15, IF, 14.5, None, OP.is_gt)
    ts(Z0, r("ROW", 0, 144), r("G15", 0, 1), None, OP.is_equal)
    ts(r("ZW", 0, 144), Z0, r("WTF", 0, 1), None, OP.mult)
    cp(r("KMF", 0, 12), r("KM", 0, 12))
    ts(r("NF", 0, 256), r("NB", 0, 256), IF, None, OP.add)
    cp(PIXW, r("NF", 0, 256))
    ts(r("IB", 0, 128), ROWM, PF, None, OP.is_equal)
    ts(r("IN", 0, 128), ROWM, PF, -1.0, OP.is_equal, OP.mult)
    ts(r("IEQ", 0, 128), ROWM, PF, VOID * 16384.0, OP.is_equal, OP.mult)
    ts(r("IDF", 0, 128), ROWM, PF, None, OP.is_equal)
    ts(r("ZD", 0, 144), Z0, FM, 16384.0, OP.mult, OP.mult)

    sent = [0]

    def send(dst, out_ap, in_reg, sem, use):
        need("g", [], [in_reg])
        rid, pid, _ = topo.addr(dst)
        m = 0
        for e in use:
            m |= 1 << e
        g.remote_dma(out_ap, ap(in_reg), T.sem[sem], T.sem["ls"], pid, rid, m)
        sent[0] += len(use)

    def lanes(src, dst):
        e = topo.engines(src, dst)
        if topo.chip(src) != topo.chip(dst):
            return e
        far = [topo.engines(src, c) for c in T.cores if topo.chip(c) != topo.chip(src)]
        rest = [k for k in e if not any(k in f for f in far)]
        return rest if rest else e

    asker = {j: T.cores[(rank - j) % N] for j in (1, 2, 3)}
    for j in (1, 2, 3):
        n = len(lanes(T.cores[(rank + j) % N], core))
        bump("rt%d" % j, n * (2 if j == 1 else 1))
        arrival([r("T%d" % j, 0, P)], ("rt%d" % j, total["rt%d" % j]))
        for (jj, t) in UPD:
            if jj == j:
                arrival([r("RU%d%d" % (j, t), 0, 32)], bump("ru%d%d" % (j, t), n))
    for i in range(2):
        c = r("TMB", 2048 * i, 2048 * i + 2048)
        act(c, c, COPY, scale=2.0)
        send(asker[1], T.T1[:, 2048 * i:2048 * i + 2048], c, "rt1", lanes(core, asker[1]))
    send(asker[2], T.T2[:, 0:P], r("TMB", 0, P), "rt2", lanes(core, asker[2]))
    send(asker[3], T.T3[:, 0:P], r("TMB", 0, P), "rt3", lanes(core, asker[3]))

    def late_constants():
        ts(r("D16", 0, 16), r("ROW", 0, 16), IF, None, OP.is_equal)
        ts(r("ROWG", 0, 128), r("ROWI", 0, 128), 4, None, OP.arith_shift_right)
        ts(r("ZE", 0, 144), Z0, FM, 2048.0, OP.mult, OP.mult)
        ts(r("ZS", 0, 144), Z0, INV15, None, OP.mult)
        ts(r("GM", 0, 128), r("ROWG", 0, 128), r("GF", 0, 1), None, OP.is_equal)
        ts(r("IVD", 0, 128), ROWM, PF, VOID * 2048.0, OP.is_equal, OP.mult)
        ts(r("I2K", 0, 128), ROWM, PF, 2048.0, OP.is_equal, OP.mult)
        ts(r("PN", 0, 256), r("NF", 0, 256), -14680064.0, None, OP.add)
        ts(r("I0", 0, 1), IF, 0.5, None, OP.is_lt)
        ts(r("PADC", 0, 1), IF, 0.5, 4096.0, OP.is_gt, OP.mult)
        tt(r("PADC", 0, 1), r("PADC", 0, 1), IF, OP.add)
        ts(r("FM2", 0, 1), FM, -1.0, 2.0, OP.mult, OP.add)

    def u_block(xb, b):
        wsum(U0[b // 2] + (b % 2) * 64, "ZW", xb, 1024 * b, 1024, True, True)

    def flip_copy(xb, first):
        x0, full = r(xb, 0, P), r(xb, FO, FO + P)
        dma("y", "sa", T.SG1[:], T[xb][15:128:16, 0:P], [r("SG1", 0, 256)], [x0])
        dma("y", "xf", ap(full), T.x[:] if first else ap(x0), [full], [] if first else [x0])
        ts(r("SG2", 0, 256), r("SG1", 0, 256), -1.0, 1.0, OP.mult, OP.add)
        dma("y", "sb", T[xb][15:128:16, FO:FO + P], T.SG2[:], [full], [r("SG2", 0, 256)])

    for b in range(4):
        u_block("XB0", b)

    ring = [0]

    def pieces(n):
        k = -(-n // BANK)
        cut = [min(n, -(-n * i // (32 * k)) * 32) for i in range(k + 1)]
        return list(zip(cut[:-1], cut[1:]))

    def run(*chains):
        chains = list(chains)
        while chains:
            chains = [c for c in chains if next(c, 0) is None]

    for t in range(4):
        X, X2 = "XB%d" % (t % 2), "XB%d" % (1 - t % 2)
        xwin = r(X, 0, P)
        tj = 1 + t % 3
        TB = "T%d" % tj

        def W(name, h, k=0):
            return r(name, 256 * k, 256 * k + 256) if h == 2 else r(name, 256 * k + HC * h, 256 * k + HC * h + HC)

        def kur(h, m):
            return r("PS", KU0 + 256 * m + HC * h, KU0 + 256 * m + HC * h + HC)

        def list_ops(h):
            cp(W("UR", h), r("PS", U0[h], U0[h] + HC))
            yield
            ts(W("U", h), W("UR", h), 4095, None, OP.bitwise_and)
            yield
            tt(W("US", h), W("U", h), W("U", h), OP.mult)
            ts(kur(h, 0), W("U", h), r("KMF", 3 * t, 3 * t + 1), None, OP.mult)
            ts(W("V1", h), W("US", h), 5, None, OP.arith_shift_right)
            yield
            for _ in q_ops(h, 0):
                yield

        def q_ops(h, m):
            if m:
                ts(kur(h, m), W("U", h), r("KMF", 3 * t + m, 3 * t + m + 1), None, OP.mult)
                yield
            tt(W("QR", h, m), kur(h, m), W("V1", h), OP.add)
            yield
            ts(W("QI", h, m), W("QR", h, m), 4095, None, OP.bitwise_and)
            yield
            cp(W("QO", h, m), W("QI", h, m))

        def q_more(m):
            tt(W("EQ", 2, m), W("QI", 2, m), PIXW, OP.is_equal)
            ts(W("QB", 2, m), W("QI", 2, m), 4096.0 * m - 16777216.0, None, OP.add)

        def d_v(h, m):
            oc, s = 256 * m + HC * h, SDT[3 * h + m]
            tt(r("AD%d" % m, s, HALF), ind(xwin, r("QO", oc + s // 16, oc + HC)), r("NX", HALF * h + s, HALF * h + HALF), OP.subtract)

        def d_s(h, m):
            todo = []
            for c, e in pieces(SDT[3 * h + m]):
                k, n = ring[0] % 2, e - c
                ring[0] += 1
                oc = 256 * m + HC * h
                act(r("XQ", 512 * k, 512 * k + n), ind(xwin, r("QO", oc + c // 16, oc + e // 16)), COPY)
                mm(ps(6 + k, 0, n), r("IB", 0, 128), r("XQ", 512 * k, 512 * k + n), True, False)
                mm(ps(6 + k, 0, n), r("IN", 0, 128), r(X, HALF * h + c, HALF * h + e), False, True)
                todo.append((c, n, k))
                if len(todo) > 1:
                    d_abs(m, todo.pop(0))
            return todo

        def d_abs(m, job):
            c, n, k = job
            act(r("AD%d" % m, c, c + n), ps(6 + k, 0, n), ACT.Abs)

        def d_vabs(h, m):
            c = r("AD%d" % m, SDT[3 * h + m], HALF)
            act(c, c, ACT.Abs)

        def d_sum(h, m):
            c = K0[h] + 128 * m
            mm(r("PS", c, c + HC), r("IDF", 0, 128), W("QB", h, m), True, False)
            mm(r("PS", c, c + HC), r("IEQ", 0, 128), W("EQ", h, m), False, False)
            wsum(c, "ZD", "AD%d" % m, 0, HALF, False, True)

        def choose(h):
            c = K0[h]
            cp(W("KA", h), r("PS", c, c + 128))
            tt(W("KB", h), r("PS", c + 128, c + 256), W("KA", h), OP.min)
            tt(W("KI", h), r("PS", c + 256, c + 384), W("KB", h), OP.min)
            ts(W("IQ", h), W("KI", h), 4095, None, OP.bitwise_and)
            cp(W("QSO", h), W("IQ", h))

        def y_v(h, c0, c1):
            c0, c1 = c0 + HALF * h, c1 + HALF * h
            tt(r("YB", c0, c1), ind(xwin, r("QSO", c0 // 16, c1 // 16)), r("NX", c0, c1), OP.add)

        def y_s(h):
            c0 = HALF * h + SY[h]
            act(r("YB", HALF * h, c0), ind(xwin, r("QSO", HC * h, c0 // 16)), COPY)

        def u_sum(h):
            wsum(UQ0[h], "ZW", "YB", HALF * h, HALF, True, True)

        def s_sum(h):
            wsum(SG0 + HC * h, "ZS", "YB", HALF * h, HALF, True, False)
            wsum(SG0 + HC * h, "ZS", X, HALF * h, SY[h], False, True)

        def h_ops(h):
            s, c = SY[h] // 16, HC * h
            cp(r("UQ", c, c + s), r("PS", UQ0[h], UQ0[h] + s))
            tt(r("UQ", c + s, c + HC), r("PS", UQ0[h] + s, UQ0[h] + HC), r("U", c + s, c + HC), OP.subtract)
            ts(W("UA", h), W("UQ", h), 4095, None, OP.bitwise_and)
            tt(W("UH", h), W("UA", h), W("U", h), OP.mult)
            ts(W("IH", h), W("UH", h), 4, 4095, OP.arith_shift_right, OP.bitwise_and)
            cp(W("HO", h), W("IH", h))

        def t_v(h, c0, c1):
            c0, c1 = c0 + HALF * h, c1 + HALF * h
            tt(r("ZB", c0, c1), ind(r(TB, 0, P), r("HO", c0 // 16, c1 // 16)), r("YB", c0, c1), OP.subtract)

        def t_s(h):
            todo = []
            for c, e in pieces(SET[h]):
                k, n = ring[0] % 2, e - c
                ring[0] += 1
                p0 = HALF * h + c
                act(r("NA", 512 * k, 512 * k + n), ind(r(TB, 0, P), r("HO", p0 // 16, (p0 + n) // 16)), COPY, scale=-1.0)
                mm(ps(6 + k, 0, n), r("IB", 0, 128), r("YB", p0, p0 + n), True, False)
                if c < SY[h]:
                    n1 = min(n, SY[h] - c)
                    mm(ps(6 + k, 0, n1), r("IB", 0, 128), r(X, p0, p0 + n1), False, False)
                mm(ps(6 + k, 0, n), r("IB", 0, 128), r("NA", 512 * k, 512 * k + n), False, True)
                todo.append((p0, n, k))
                if len(todo) > 1:
                    t_abs(todo.pop(0))
            return todo

        def t_abs(job):
            p0, n, k = job
            act(r("ZB", p0, p0 + n), ps(6 + k, 0, n), ACT.Abs)

        def t_vabs(h, c0, c1):
            act(r("ZB", HALF * h + c0, HALF * h + c1), r("ZB", HALF * h + c0, HALF * h + c1), ACT.Abs)

        def e_head(h):
            w0, w1 = HC * h, HC * h + HC
            o = r("PS", KEY + w0, KEY + w1)
            mm(o, r("IDF", 0, 128), r("PN", w0, w1), True, False)
            mm(o, r("I2K", 0, 128), r("KF", w0, w1), False, False)
            mm(o, r("IVD", 0, 128), r("VD", w0, w1), False, False)

        def e_sum(h, c0, c1):
            wsum(KEY + HC * h + c0 // 16, "ZE", "ZB", HALF * h + c0, c1 - c0, False, c1 == HALF)

        if t:
            act(r("NX", NXC[0], HALF), r(X, NXC[0], HALF), COPY)
            c = r("NX", NXC[1], P)
            dma("y", "nx1", ap(c), T[X][:, NXC[1]:P], [c], [r(X, NXC[1], P)])
        run(list_ops(0))
        pend = None
        for n, (h, m) in enumerate([(h, m) for h in (0, 1) for m in (0, 1, 2)]):
            left = d_s(h, m)
            if pend is not None:
                d_vabs(*pend)
            for job in left:
                d_abs(m, job)
            if n == 1:
                q_more(0)
                q_more(1)
            elif n == 2:
                q_more(2)
            if pend is not None:
                d_sum(*pend)
            pend = (h, m)
            if n == 0:
                d_v(0, 0)
                run(list_ops(1), q_ops(0, 1))
                d_v(0, 1)
                run(q_ops(0, 2), q_ops(1, 1), q_ops(1, 2))
            elif n == 1:
                d_v(0, 2)
            elif n == 2:
                if t == 0:
                    late_constants()
            else:
                d_v(h, m)
                if n == 3:
                    flip_copy(X, t == 0)
                if n == 4:
                    choose(0)
        d_vabs(1, 2)
        d_sum(1, 2)
        y_s(0)
        y_v(0, SY[0], HALF)
        u_sum(0)
        s_sum(0)
        choose(1)
        y_s(1)
        y_v(1, SY[1], YC)
        for (j, tu) in UPD:
            if j == tj and tu < t:
                RU = "RU%d%d" % (j, tu)
                cp(r("OFF", 8 + 2 * tu, 9 + 2 * tu), r(RU, 16, 17))
                cp(ind(r(TB, 0, P + 16), r("OFF", 8 + 2 * tu, 9 + 2 * tu)), r(RU, 0, 16))
        h_ops(0)
        y_v(1, YC, HALF)
        mid = (SET[0] + HALF) // 2 // 32 * 32
        left = t_s(0)
        u_sum(1)
        ts(W("KD", 2), W("KI", 2), 14, None, OP.arith_shift_right)
        t_v(0, SET[0], mid)
        cp(W("KF", 2), W("KD", 2))
        ts(W("VD", 2), W("KD", 2), VOID - 1024.0, None, OP.is_ge)
        e_head(0)
        e_head(1)
        h_ops(1)
        t_v(0, mid, HALF)
        s_sum(1)
        for job in left:
            t_abs(job)
        t_vabs(0, SET[0], mid)
        left = t_s(1)
        t_vabs(0, mid, HALF)
        e_sum(0, 0, HALF)
        for job in left:
            t_abs(job)
        cuts = [SET[1], CUT[0], CUT[1], HALF]
        for c0, c1 in zip(cuts[:-1], cuts[1:]):
            t_v(1, c0, c1)
            t_vabs(1, c0, c1)
        e_sum(1, 0, CUT[0])
        e_sum(1, CUT[0], HALF)
        red(cf(0), r("PS", KEY, KEY + HC))
        ts(r("R32", 0, 16), r("D16", 0, 16), cf(0), None, OP.mult)
        tt(ps(2, 0, 256), W("IQ", 2), PIXW, OP.min)
        ts(W("DIRT", 2), r("PS", SG0, SG0 + 256), 1.0, None, OP.not_equal)
        tt(W("CC", 2), ps(2, 0, 256), W("DIRT", 2), OP.mult)
        red(cf(1), r("PS", KEY + HC, KEY + 2 * HC))
        ts(r("R32", 16, 32), r("D16", 0, 16), cf(1), None, OP.mult)

        s1, s2 = SMALL1, SMALL2
        mm(r("PS", s1, s1 + 32), r("GM", 0, 128), r("R32", 0, 32), True, True)
        kk = r("CI", 0, 1)
        red(kk, r("PS", s1, s1 + 32))
        ts(r("CI", 1, 2), kk, 4, 255, OP.arith_shift_right, OP.bitwise_and)
        ts(r("CI", 2, 3), kk, 15, None, OP.bitwise_and)
        cp(r("OFF", 0, 1), r("CI", 1, 2))
        tt(cf(2), r("II", 0, 1), r("CI", 2, 3), OP.is_equal)
        ts(r("CI", 3, 4), kk, 4095, None, OP.bitwise_and)
        for n, w in enumerate(["IQ", "DIRT", "IH"]):
            ts(r("GQ", 16 * n, 16 * n + 16), ind(r(w, 0, 256), r("OFF", 0, 1)), cf(2), None, OP.mult)
        mm(r("PS", s2, s2 + 48), r("GM", 0, 128), r("GQ", 0, 48), True, True)
        cp(cf(3), r("CI", 3, 4))
        q1, dirc, hc = r("PS", s2, s2 + 1), r("PS", s2 + 16, s2 + 17), r("PS", s2 + 32, s2 + 33)
        a, b = cf(6), cf(7)
        ts(cf(4), q1, cf(3), 0.5, OP.min, OP.add)
        ts(cf(5), q1, cf(3), -0.5, OP.max, OP.add)
        ts(CLAMP, r("CC", 0, 256), cf(4), cf(5), OP.max, OP.min)
        ts(a, q1, cf(3), None, OP.min)
        ts(b, q1, cf(3), None, OP.max)
        tt(r("NN", 0, 256), CLAMP, r("CC", 0, 256), OP.is_equal)
        ts(r("OFF", 2, 3), q1, cf(3), None, OP.min)
        ts(r("OFF", 4, 5), q1, cf(3), None, OP.max)
        tt(r("K2", 0, 256), r("PS", KEY, KEY + 256), r("NN", 0, 256), OP.mult)
        if t < 3:
            ts(r("UP%d" % t, 16, 17), hc, r("I0", 0, 1), r("PADC", 0, 1), OP.mult, OP.add)
        cp(cf(8), dirc)
        mm(YSUM, r("IDF", 0, 128), r("NF", 0, 256), True, False)
        red(cf(0), r("K2", 0, 256))
        act(cf(9), cf(8), COPY, scale=-1.0, bias=1.0)
        act(cf(10), a, COPY, bias=b)
        act(cf(18), cf(9), COPY, scale=FO + 1.0)
        act(cf(12), a, COPY, scale=-1.0, bias=b)
        act(cf(11), cf(10), COPY, scale=cf(9), bias=cf(18))
        act(cf(32), cf(12), COPY, scale=cf(8))
        act(cf(19), cf(11), COPY, scale=-1.0)
        act(cf(13), cf(12), COPY, scale=cf(8), bias=cf(19))
        act(cf(20), cf(9), COPY, scale=4095.0)
        act(cf(21), b, COPY, scale=cf(8), bias=cf(20))
        act(cf(25), cf(32), COPY, scale=-1.0)
        act(r("XA", 0, 16), ind(xwin, r("OFF", 2, 3)), COPY, scale=r("FM2", 0, 1))
        act(r("XC", 0, 16), ind(xwin, r("OFF", 4, 5)), COPY, scale=FM)
        ts(r("R32", 0, 16), r("D16", 0, 16), cf(0), None, OP.mult)
        mm(r("PS", s1, s1 + 16), r("GM", 0, 128), r("R32", 0, 16), True, True)
        ts(r("OFF", 6, 7), a, r("I0", 0, 1), r("PADC", 0, 1), OP.mult, OP.add)
        kk = r("CI", 4, 5)
        red(kk, r("PS", s1, s1 + 16))
        ts(r("CI", 5, 6), kk, 4, 255, OP.arith_shift_right, OP.bitwise_and)
        ts(r("CI", 6, 7), kk, 15, None, OP.bitwise_and)
        cp(r("OFF", 0, 1), r("CI", 5, 6))
        tt(cf(33), r("II", 0, 1), r("CI", 6, 7), OP.is_equal)
        ts(r("CI", 7, 8), kk, 4095, None, OP.bitwise_and)
        ts(r("GQ", 48, 64), ind(r("IQ", 0, 256), r("OFF", 0, 1)), cf(33), None, OP.mult)
        mm(r("PS", s2, s2 + 16), r("GM", 0, 128), r("GQ", 48, 64), True, True)
        ts(cf(15), kk, 0.0, cf(8), OP.is_lt, OP.mult)
        ts(r("Y0", 0, 256), r("NF", 0, 256), a, cf(13), OP.is_gt, OP.mult)
        mm(YSUM, r("IDF", 0, 128), r("Y0", 0, 256), False, False)
        cp(cf(14), r("CI", 7, 8))
        ts(cf(16), cf(15), -8192.0, 8192.0, OP.mult, OP.add)
        tt(r("NI", 0, 16), r("XA", 0, 16), r("XC", 0, 16), OP.add)
        tt(cf(17), cf(16), b, OP.add)
        ts(r("Y1", 0, 256), r("NF", 0, 256), b, cf(11), OP.is_gt, OP.mult)
        mm(YSUM, r("IDF", 0, 128), r("Y1", 0, 256), False, True)
        act(r("VA", 0, 256), YSUM, ACT.Abs)
        q2 = r("PS", s2, s2 + 1)
        d, L = cf(27), cf(28)
        ts(cf(22), q2, cf(14), cf(17), OP.max, OP.is_gt)
        ts(cf(23), q2, cf(14), cf(21), OP.min, OP.subtract)
        ts(cf(24), q2, cf(14), 4095.0, OP.max, OP.subtract)
        ts(cf(26), cf(23), cf(22), cf(21), OP.mult, OP.add)
        ts(d, cf(24), cf(22), 4095.0, OP.mult, OP.add)
        ts(r("NJ", 0, 16), r("NI", 0, 16), 1, None, OP.arith_shift_right)
        tt(L, d, cf(26), OP.subtract)
        tt(cf(29), d, cf(12), OP.subtract)
        cp(ind(r(X, 0, P + 16), r("OFF", 6, 7)), r("NJ", 0, 16))
        tt(cf(31), L, a, OP.add)
        ts(cf(30), L, -1.0, None, OP.mult)

        o1, o2 = [[ps(4 + k, HC * h, HC * h + HC) for h in (0, 1)] for k in (0, 1)]
        o3 = [r("PS", K0[h], K0[h] + HC) for h in (0, 1)]
        both = (0, 1)
        for h in both:
            ts(o1[h], W("NF", h), d, L, OP.is_gt, OP.mult)
            ts(W("TB", h), W("NF", h), cf(31), cf(25), OP.is_gt, OP.mult)
        for h in both:
            ts(o2[h], W("NF", h), cf(29), cf(30), OP.is_gt, OP.mult)
            tt(W("TA", h), o1[h], W("TB", h), OP.add)
        for h in both:
            tt(o3[h], o2[h], W("TA", h), OP.add)
        for h in both:
            tt(W("TC", h), o3[h], W("VA", h), OP.add)
        for h in both:
            cp(W("RO", h), W("TC", h))
        for n, (c0, c1, q) in enumerate(MOVE):
            src = ind(r(X, 0, XW), r("RO", c0 // 16, c1 // 16))
            if q == "s":
                act(r(X2, c0, c1), src, COPY)
            else:
                cp(r(X2, c0, c1), src)
            if t == 3:
                dma("y", "y%d" % n, T.y[:, c0:c1], T[X2][:, c0:c1], [], [r(X2, c0, c1)])
        if t < 3:
            for bl in range(4):
                u_block(X2, bl)
            ts(r("UP%d" % t, 0, 16), r("NJ", 0, 16), 2.0, None, OP.mult)
            for (j, tu) in UPD:
                if tu == t:
                    send(asker[j], T["RU%d%d" % (j, t)][:], r("UP%d" % t, 0, 32), "ru%d%d" % (j, t), lanes(core, asker[j]))

    total["ls"] = sent[0]
    for sem, val in total.items():
        if clock["g"].get(sem, 0) < val:
            g.wait_ge(T.sem[sem], val)
